import numpy as np
import ml_dtypes


def mxq(x, axis, fmt="e4m3"):
    dtype, down = {"e4m3": (ml_dtypes.float8_e4m3fn, 7), "e5m2": (ml_dtypes.float8_e5m2, 14)}[fmt]
    v = np.moveaxis(np.asarray(x, np.float32).astype(ml_dtypes.bfloat16).astype(np.float64), axis, -1)
    blocks = v.reshape(v.shape[:-1] + (-1, 32))
    amax = np.abs(blocks).max(-1, keepdims=True)
    byte = np.maximum(np.where(amax > 0, np.frexp(amax)[1] - 1 + 127, 0) - down, 1)
    scale = np.exp2(byte - 127.0)
    codes = (blocks / scale).astype(np.float32).astype(dtype).astype(np.float64)
    return np.moveaxis((codes * scale).reshape(v.shape), -1, axis)


WIDE = False


def mx_kscale(k):
    if not WIDE:
        return np.ones(k)
    levels = np.array([10, -10, 5, -5, 0])
    if k % 512:
        return np.exp2(np.random.permutation(np.resize(levels, k // 32))).repeat(32)
    a = np.empty((k // 512, 16))
    for p in range(k // 512):
        a[p, :8] = np.random.permutation(np.resize(levels, 8))
        for g in range(8):
            far = levels[np.abs(levels - a[p, g]) >= 10]
            a[p, g + 8] = far[np.random.randint(len(far))]
    return np.exp2(a.ravel()).repeat(32)


def f64(x):
    return np.asarray(x).astype(np.float64)


def striped(idx):
    return np.tile(np.asarray(idx).reshape(-1, 16).T, (8, 1)).astype(np.uint16)


def unstriped(offs):
    return offs[:16].T.reshape(-1).astype(np.int64)


E, T, I, J = 512, 1024, 512, 512


def setup_inputs():
    n = np.random.standard_normal
    idx = np.random.permutation(T)[:I]
    idx2 = np.random.permutation(T)[:J]
    fi = mx_kscale(I)
    ti = np.ones(T)
    ti[idx] = fi
    return {
        "first": (n((E, T))).astype(np.float32),
        "second": (n((E, T)) / ti).astype(np.float32),
        "ws": (n((I, J)) * 1 / np.sqrt(I) * fi[:, None]).astype(np.float32),
        "bias": (1.0 * n((J, 1))).astype(np.float32),
        "offs": striped(idx),
        "offs2": striped(idx2),
    }


def reference(first, second, ws, bias, offs, offs2):
    idx = unstriped(offs)
    idx2 = unstriped(offs2)
    vt = f64(second)[:, idx].T
    wsq = mxq(f64(ws), 0, "e4m3")
    vtq = mxq(vt, 0, "e4m3")
    v = wsq.T @ vtq
    ut = f64(first)[:, idx2].T
    y = ut * (v + f64(bias))
    return y

@@ -1,0 +1,128 @@
+from contextlib import ExitStack
+
+import concourse.mybir as mybir
+from concourse.masks import make_identity
+
+E, T, I, J = 512, 1024, 512, 512
+FLOPS = 2 * I * J * E
+
+F32 = mybir.dt.float32
+BF16 = mybir.dt.bfloat16
+U32 = mybir.dt.uint32
+U16 = mybir.dt.uint16
+U8 = mybir.dt.uint8
+FP8X4 = mybir.dt.float8_e4m3fn_x4
+ADD = mybir.AluOpType.add
+MULT = mybir.AluOpType.mult
+
+P = 128
+PACK = 4
+EB = E // P
+JB = J // P
+HALF = J // 2
+
+
+def tile_attend_spatialgate_kernel(tc, first, second, ws, bias, offs, offs2, out):
+    nc = tc.nc
+    with ExitStack() as ctx:
+        keep = ctx.enter_context(tc.tile_pool(name="keep", bufs=1))
+        turn = ctx.enter_context(tc.psum_pool(name="turn", bufs=4))
+        acc = ctx.enter_context(tc.psum_pool(name="acc", bufs=4))
+
+        slots = keep.tile([P, I // 16], U16, name="slots")
+        places = keep.tile([P, J // 16], U16, name="places")
+        s_win = [keep.tile([P, T], F32, name=f"s_win{b}") for b in range(EB)]
+        f_win = [keep.tile([P, T], F32, name=f"f_win{b}") for b in range(EB)]
+        w_raw = [keep.tile([P, PACK, HALF], F32, name=f"w_raw{h}") for h in range(2)]
+        w_rows = ws.rearrange("(p t) j -> p t j", t=PACK)
+
+        ident = keep.tile([P, P], F32, name="ident")
+        make_identity(nc, ident[:])
+        bias_rows = keep.tile([P, P], F32, name="bias_rows")
+        nc.gpsimd.memset(bias_rows[:], 0.0)
+
+        def load(tile, src, b):
+            nc.sync.dma_start(tile[b][:], src[b * P : (b + 1) * P, :])
+
+        def load_w(h):
+            nc.sync.dma_start(w_raw[h][:], w_rows[:, :, h * HALF : (h + 1) * HALF])
+
+        load(s_win, second, 0)
+        nc.sync.dma_start(slots[:], offs)
+        for b in range(1, EB):
+            load(s_win, second, b)
+        load(f_win, first, 0)
+        nc.sync.dma_start(places[:], offs2)
+        load(f_win, first, 1)
+        load(f_win, first, 2)
+        load_w(0)
+        load(f_win, first, 3)
+        load_w(1)
+        nc.scalar.dma_start(bias_rows[0:JB, :], bias.rearrange("(b p) o -> b (p o)", p=P))
+
+        bias_ps = turn.tile([P, 4, P], F32, name="turned")
+        nc.tensor.transpose(bias_ps[:, 0, :], bias_rows[:], ident[:])
+        bias_col = keep.tile([P, JB], F32, name="bias_col")
+        nc.scalar.copy(bias_col[:], bias_ps[:, 0, 0:JB])
+
+        vt_codes = keep.tile([P, E], U32, name="vt_codes", align_bytes=64)
+        vt_scales = keep.tile([P, E], U8, name="vt_scales", align_bytes=64)
+        vt_woven = [keep.tile([P, 2 * P * PACK], BF16, name=f"vt_woven{h}", align_bytes=64) for h in range(2)]
+        for b in range(EB):
+            picked = keep.tile([P, I], BF16, name=f"s_picked{b}")
+            nc.vector.tensor_copy(picked[:], s_win[b][:].indirect(slots[:]))
+            words = picked[:].bitcast(F32)
+            turned = turn.tile([P, 4, P], F32, name="turned")
+            for u in range(2):
+                nc.tensor.transpose(turned[:, u, :], words[:, u : I // 2 : 2], ident[:])
+            dst = vt_woven[b // 2][:].bitcast(F32)[:, (b % 2) * 2 * P : (b % 2 + 1) * 2 * P]
+            nc.scalar.copy(dst.rearrange("p (e u) -> p e u", u=2), turned[:, 0:2, :].rearrange("p u e -> p e u"))
+            if b % 2 == 1:
+                cols = slice((b - 1) * P, (b + 1) * P)
+                nc.vector.quantize_mx(vt_codes[:, cols].bitcast(FP8X4), vt_scales[:, cols], vt_woven[b // 2][:])
+
+        ut = keep.tile([P, JB, E], F32, name="ut")
+
+        def first_part(b, j0, j1):
+            picked = keep.tile([P, (j1 - j0) * P], F32, name=f"f_picked{b}_{j0}")
+            nc.vector.tensor_copy(picked[:], f_win[b][:].indirect(places[:, j0 * 8 : j1 * 8]))
+            turned = turn.tile([P, 4, P], F32, name="turned")
+            for jb in range(j0, j1):
+                nc.tensor.transpose(turned[:, jb, :], picked[:, (jb - j0) * P : (jb - j0 + 1) * P], ident[:])
+            nc.scalar.copy(ut[:, j0:j1, b * P : (b + 1) * P], turned[:, j0:j1, :])
+
+        sums = {}
+
+        def weights(jb):
+            woven = keep.tile([P, P * PACK], BF16, name=f"w_woven{jb}", align_bytes=64)
+            src = w_raw[jb // 2][:, :, (jb % 2) * P : (jb % 2 + 1) * P]
+            nc.scalar.copy(
+                woven[:].rearrange("p (c i t) -> p c t i", i=4, t=PACK),
+                src.rearrange("p t (c i) -> p c t i", i=4),
+            )
+            codes = keep.tile([P, P], U32, name=f"w_codes{jb}", align_bytes=64)
+            scales = keep.tile([P, P], U8, name=f"w_scales{jb}", align_bytes=64)
+            nc.vector.quantize_mx(codes[:].bitcast(FP8X4), scales[:], woven[:])
+            sums[jb] = acc.tile([P, E], F32, name="sums")
+            nc.tensor.matmul_mx(
+                sums[jb][:], lhsT=codes[:].bitcast(FP8X4), lhsT_scale=scales[:],
+                rhs=vt_codes[:].bitcast(FP8X4), rhs_scale=vt_scales[:], start=True, stop=True,
+            )
+
+        def finish(jb):
+            res = keep.tile([P, E], F32, name=f"res{jb}")
+            nc.vector.scalar_tensor_tensor(res[:], sums[jb][:], bias_col[:, jb : jb + 1], ut[:, jb, :], ADD, MULT)
+            nc.sync.dma_start(out[jb * P : (jb + 1) * P, :], res[:])
+
+        for b in range(3):
+            first_part(b, 0, JB)
+        weights(0)
+        first_part(3, 0, 2)
+        weights(1)
+        first_part(3, 2, 4)
+        weights(2)
+        finish(0)
+        weights(3)
+        finish(1)
+        finish(2)
+        finish(3)

@@ -12,117 +12,166 @@ U32 = mybir.dt.uint32
 U16 = mybir.dt.uint16
 U8 = mybir.dt.uint8
 FP8X4 = mybir.dt.float8_e4m3fn_x4
-ADD = mybir.AluOpType.add
 MULT = mybir.AluOpType.mult
+IDENTITY = mybir.ActivationFunctionType.Identity
 
 P = 128
 PACK = 4
+LINE = 4
+ENTRIES = 16
+BANK = 512
 EB = E // P
 JB = J // P
-HALF = J // 2
+HALF = 256
 
 
 def tile_attend_spatialgate_kernel(tc, first, second, ws, bias, offs, offs2, out):
     nc = tc.nc
     with ExitStack() as ctx:
         keep = ctx.enter_context(tc.tile_pool(name="keep", bufs=1))
-        turn = ctx.enter_context(tc.psum_pool(name="turn", bufs=4))
-        acc = ctx.enter_context(tc.psum_pool(name="acc", bufs=4))
+        rotating = ctx.enter_context(tc.psum_pool(name="rotating", bufs=4))
+        held = ctx.enter_context(tc.psum_pool(name="held", bufs=1))
 
-        slots = keep.tile([P, I // 16], U16, name="slots")
-        places = keep.tile([P, J // 16], U16, name="places")
-        s_win = [keep.tile([P, T], F32, name=f"s_win{b}") for b in range(EB)]
-        f_win = [keep.tile([P, T], F32, name=f"f_win{b}") for b in range(EB)]
-        w_raw = [keep.tile([P, PACK, HALF], F32, name=f"w_raw{h}") for h in range(2)]
-        w_rows = ws.rearrange("(p t) j -> p t j", t=PACK)
+        slots = keep.tile([P, I // ENTRIES], U16, name="slots")
+        places = keep.tile([P, J // ENTRIES], U16, name="places")
+        second_sb = [keep.tile([P, T], F32, name=f"second{b}") for b in range(EB)]
+        first_sb = [keep.tile([P, T], F32, name=f"first{b}") for b in range(EB)]
+        ws_sb = [keep.tile([P, PACK, HALF], F32, name=f"ws{g}", tag=f"ws{g}") for g in range(2)]
+        ws_rows = ws.rearrange("(p t) j -> p t j", t=PACK)
 
-        ident = keep.tile([P, P], F32, name="ident")
-        make_identity(nc, ident[:])
         bias_rows = keep.tile([P, P], F32, name="bias_rows")
         nc.gpsimd.memset(bias_rows[:], 0.0)
+        ident = keep.tile([P, P], F32, name="ident")
+        make_identity(nc, ident[:])
 
-        def load(tile, src, b):
-            nc.sync.dma_start(tile[b][:], src[b * P : (b + 1) * P, :])
+        def load_block(tiles, src, b):
+            nc.sync.dma_start(tiles[b][:], src[b * P : (b + 1) * P, :])
 
-        def load_w(h):
-            nc.sync.dma_start(w_raw[h][:], w_rows[:, :, h * HALF : (h + 1) * HALF])
-
-        load(s_win, second, 0)
+        load_block(second_sb, second, 0)
         nc.sync.dma_start(slots[:], offs)
         for b in range(1, EB):
-            load(s_win, second, b)
-        load(f_win, first, 0)
+            load_block(second_sb, second, b)
+        load_block(first_sb, first, 0)
         nc.sync.dma_start(places[:], offs2)
-        load(f_win, first, 1)
-        load(f_win, first, 2)
-        load_w(0)
-        load(f_win, first, 3)
-        load_w(1)
+        for g in range(2):
+            nc.sync.dma_start(ws_sb[g][:], ws_rows[:, :, g * HALF : (g + 1) * HALF])
+        for b in range(1, EB):
+            load_block(first_sb, first, b)
         nc.scalar.dma_start(bias_rows[0:JB, :], bias.rearrange("(b p) o -> b (p o)", p=P))
 
-        bias_ps = turn.tile([P, 4, P], F32, name="turned")
-        nc.tensor.transpose(bias_ps[:, 0, :], bias_rows[:], ident[:])
+        width = {"vt": E, "ws0": HALF, "ws1": HALF}
+        woven = {n: keep.tile([P, width[n] * PACK], BF16, name=f"{n}_woven", align_bytes=64) for n in width}
+        codes = {n: keep.tile([P, width[n]], U32, name=f"{n}_codes", align_bytes=64) for n in width}
+        scales = {n: keep.tile([P, width[n]], U8, name=f"{n}_scales", align_bytes=64) for n in width}
+        gate = {(h, g): held.tile([P, BANK], F32, name=f"gate{h}{g}") for h in range(2) for g in range(2)}
+        biased = {k: keep.tile([P, BANK], F32, name=f"biased{k[0]}{k[1]}") for k in gate}
+
+        nc.tensor.transpose(gate[1, 1][:, 0:P], bias_rows[:], ident[:])
         bias_col = keep.tile([P, JB], F32, name="bias_col")
-        nc.scalar.copy(bias_col[:], bias_ps[:, 0, 0:JB])
+        nc.scalar.activation(bias_col[:], gate[1, 1][:, 0:JB], IDENTITY)
+        out_v = out.rearrange("(b p) e -> p b e", p=P)
 
-        vt_codes = keep.tile([P, E], U32, name="vt_codes", align_bytes=64)
-        vt_scales = keep.tile([P, E], U8, name="vt_scales", align_bytes=64)
-        vt_woven = [keep.tile([P, 2 * P * PACK], BF16, name=f"vt_woven{h}", align_bytes=64) for h in range(2)]
-        for b in range(EB):
-            picked = keep.tile([P, I], BF16, name=f"s_picked{b}")
-            nc.vector.tensor_copy(picked[:], s_win[b][:].indirect(slots[:]))
+        def quantise(name):
+            nc.vector.quantize_mx(codes[name][:].bitcast(FP8X4), scales[name][:], woven[name][:])
+
+        def pick_second(b):
+            picked = keep.tile([P, I], BF16, name=f"second_picked{b}")
+            nc.vector.tensor_copy(picked[:], second_sb[b][:].indirect(slots[:]))
             words = picked[:].bitcast(F32)
-            turned = turn.tile([P, 4, P], F32, name="turned")
+            turned = rotating.tile([P, BANK], F32, name="bank")
             for u in range(2):
-                nc.tensor.transpose(turned[:, u, :], words[:, u : I // 2 : 2], ident[:])
-            dst = vt_woven[b // 2][:].bitcast(F32)[:, (b % 2) * 2 * P : (b % 2 + 1) * 2 * P]
-            nc.scalar.copy(dst.rearrange("p (e u) -> p e u", u=2), turned[:, 0:2, :].rearrange("p u e -> p e u"))
-            if b % 2 == 1:
-                cols = slice((b - 1) * P, (b + 1) * P)
-                nc.vector.quantize_mx(vt_codes[:, cols].bitcast(FP8X4), vt_scales[:, cols], vt_woven[b // 2][:])
-
-        ut = keep.tile([P, JB, E], F32, name="ut")
-
-        def first_part(b, j0, j1):
-            picked = keep.tile([P, (j1 - j0) * P], F32, name=f"f_picked{b}_{j0}")
-            nc.vector.tensor_copy(picked[:], f_win[b][:].indirect(places[:, j0 * 8 : j1 * 8]))
-            turned = turn.tile([P, 4, P], F32, name="turned")
-            for jb in range(j0, j1):
-                nc.tensor.transpose(turned[:, jb, :], picked[:, (jb - j0) * P : (jb - j0 + 1) * P], ident[:])
-            nc.scalar.copy(ut[:, j0:j1, b * P : (b + 1) * P], turned[:, j0:j1, :])
-
-        sums = {}
-
-        def weights(jb):
-            woven = keep.tile([P, P * PACK], BF16, name=f"w_woven{jb}", align_bytes=64)
-            src = w_raw[jb // 2][:, :, (jb % 2) * P : (jb % 2 + 1) * P]
+                nc.tensor.transpose(turned[:, u * P : (u + 1) * P], words[:, u : I // 2 : 2], ident[:])
+            dst = woven["vt"][:].bitcast(F32)[:, b * 2 * P : (b + 1) * 2 * P]
             nc.scalar.copy(
-                woven[:].rearrange("p (c i t) -> p c t i", i=4, t=PACK),
-                src.rearrange("p t (c i) -> p c t i", i=4),
-            )
-            codes = keep.tile([P, P], U32, name=f"w_codes{jb}", align_bytes=64)
-            scales = keep.tile([P, P], U8, name=f"w_scales{jb}", align_bytes=64)
-            nc.vector.quantize_mx(codes[:].bitcast(FP8X4), scales[:], woven[:])
-            sums[jb] = acc.tile([P, E], F32, name="sums")
-            nc.tensor.matmul_mx(
-                sums[jb][:], lhsT=codes[:].bitcast(FP8X4), lhsT_scale=scales[:],
-                rhs=vt_codes[:].bitcast(FP8X4), rhs_scale=vt_scales[:], start=True, stop=True,
+                dst.rearrange("p (e u) -> p e u", u=2), turned[:, 0 : 2 * P].rearrange("p (u e) -> p e u", u=2)
             )
 
-        def finish(jb):
-            res = keep.tile([P, E], F32, name=f"res{jb}")
-            nc.vector.scalar_tensor_tensor(res[:], sums[jb][:], bias_col[:, jb : jb + 1], ut[:, jb, :], ADD, MULT)
-            nc.sync.dma_start(out[jb * P : (jb + 1) * P, :], res[:])
+        def weave_ws(g):
+            nc.scalar.copy(
+                woven[f"ws{g}"][:].rearrange("p (c i t) -> p c t i", i=LINE, t=PACK),
+                ws_sb[g][:].rearrange("p t (c i) -> p c t i", i=LINE),
+            )
 
-        for b in range(3):
-            first_part(b, 0, JB)
-        weights(0)
-        first_part(3, 0, 2)
-        weights(1)
-        first_part(3, 2, 4)
-        weights(2)
-        finish(0)
-        weights(3)
-        finish(1)
-        finish(2)
-        finish(3)
+        def mix(h, g):
+            sums = rotating.tile([P, BANK], F32, name="bank")
+            features = slice(h * HALF, (h + 1) * HALF)
+            for s in range(2):
+                block = slice(s * P, (s + 1) * P)
+                nc.tensor.matmul_mx(
+                    sums[:, s * HALF : (s + 1) * HALF],
+                    lhsT=codes[f"ws{g}"][:, block].bitcast(FP8X4),
+                    lhsT_scale=scales[f"ws{g}"][:, block],
+                    rhs=codes["vt"][:, features].bitcast(FP8X4),
+                    rhs_scale=scales["vt"][:, features],
+                    start=True,
+                    stop=True,
+                )
+            for s in range(2):
+                cols = slice(s * HALF, (s + 1) * HALF)
+                jb = 2 * g + s
+                nc.scalar.activation(biased[h, g][:, cols], sums[:, cols], IDENTITY, bias=bias_col[:, jb : jb + 1])
+
+        def pick_first(b, jb0, jb1):
+            picked = keep.tile([P, (jb1 - jb0) * P], F32, name=f"first_picked{b}_{jb0}")
+            entries = places[:, jb0 * P // ENTRIES : jb1 * P // ENTRIES]
+            nc.vector.tensor_copy(picked[:], first_sb[b][:].indirect(entries))
+            for jb in range(jb0, jb1):
+                c0 = (jb % 2) * HALF + (b % 2) * P
+                src = picked[:, (jb - jb0) * P : (jb - jb0 + 1) * P]
+                nc.tensor.transpose(gate[b // 2, jb // 2][:, c0 : c0 + P], src, ident[:])
+
+        low_res = {g: keep.tile([P, 2, 2, P], F32, name=f"low_res{g}") for g in range(2)}
+
+        def piece(tile, b):
+            return tile[:].rearrange("p (s b e) -> p s b e", s=2, b=2)[:, :, b, :]
+
+        def finish_low(engine, g, b, ut):
+            engine.tensor_tensor(low_res[g][:, :, b, :], ut, piece(biased[0, g], b), MULT)
+
+        def store_low(queue, g, b):
+            queue.dma_start(out_v[:, 2 * g : 2 * g + 2, b * P : (b + 1) * P], low_res[g][:, :, b, :])
+
+        def finish_high(jb):
+            g, s = divmod(jb, 2)
+            cols = slice(s * HALF, (s + 1) * HALF)
+            res = keep.tile([P, HALF], F32, name=f"high_res{jb}")
+            nc.vector.tensor_tensor(res[:], gate[1, g][:, cols], biased[1, g][:, cols], MULT)
+            nc.sync.dma_start(out_v[:, jb : jb + 1, HALF:E], res[:].rearrange("p (s e) -> p s e", e=HALF))
+
+        for b in range(EB):
+            pick_second(b)
+        pick_first(0, 0, JB)
+        quantise("vt")
+        weave_ws(0)
+        weave_ws(1)
+
+        ut_block0 = keep.tile([P, 2, 2, P], F32, name="ut_block0", tag="ws1")
+        for g in range(2):
+            nc.scalar.copy(ut_block0[:, g, :, :], piece(gate[0, g], 0))
+
+        quantise("ws0")
+        mix(0, 0)
+        finish_low(nc.gpsimd, 0, 0, ut_block0[:, 0, :, :])
+        store_low(nc.sync, 0, 0)
+        mix(1, 0)
+
+        pick_first(1, 0, JB)
+        ut_block1 = keep.tile([P, 2, P], F32, name="ut_block1")
+        nc.scalar.copy(ut_block1[:], piece(gate[0, 0], 1))
+        finish_low(nc.gpsimd, 0, 1, ut_block1[:])
+        store_low(nc.sync, 0, 1)
+
+        quantise("ws1")
+        mix(0, 1)
+        finish_low(nc.gpsimd, 1, 0, ut_block0[:, 1, :, :])
+        mix(1, 1)
+
+        pick_first(2, 0, JB)
+        pick_first(3, 0, JB // 2)
+        pick_first(3, JB // 2, JB)
+        finish_low(nc.vector, 1, 1, piece(gate[0, 1], 1))
+        store_low(nc.sync, 1, 1)
+        finish_high(0)
+        store_low(nc.scalar, 1, 0)
+        for jb in range(1, JB):
+            finish_high(jb)

from contextlib import ExitStack

import concourse.mybir as mybir
from concourse.masks import make_identity

E, T, I, J = 512, 1024, 512, 512
FLOPS = 2 * I * J * E

F32 = mybir.dt.float32
BF16 = mybir.dt.bfloat16
U32 = mybir.dt.uint32
U16 = mybir.dt.uint16
U8 = mybir.dt.uint8
FP8X4 = mybir.dt.float8_e4m3fn_x4
MULT = mybir.AluOpType.mult
IDENTITY = mybir.ActivationFunctionType.Identity

P = 128
PACK = 4
LINE = 4
ENTRIES = 16
BANK = 512
EB = E // P
JB = J // P
HALF = 256


def tile_attend_spatialgate_kernel(tc, first, second, ws, bias, offs, offs2, out):
    nc = tc.nc
    with ExitStack() as ctx:
        keep = ctx.enter_context(tc.tile_pool(name="keep", bufs=1))
        rotating = ctx.enter_context(tc.psum_pool(name="rotating", bufs=4))
        held = ctx.enter_context(tc.psum_pool(name="held", bufs=1))

        slots = keep.tile([P, I // ENTRIES], U16, name="slots")
        places = keep.tile([P, J // ENTRIES], U16, name="places")
        second_sb = [keep.tile([P, T], F32, name=f"second{b}") for b in range(EB)]
        first_sb = [keep.tile([P, T], F32, name=f"first{b}") for b in range(EB)]
        ws_sb = [keep.tile([P, PACK, HALF], F32, name=f"ws{g}", tag=f"ws{g}") for g in range(2)]
        ws_rows = ws.rearrange("(p t) j -> p t j", t=PACK)

        bias_rows = keep.tile([P, P], F32, name="bias_rows")
        nc.gpsimd.memset(bias_rows[:], 0.0)
        ident = keep.tile([P, P], F32, name="ident")
        make_identity(nc, ident[:])

        def load_block(tiles, src, b):
            nc.sync.dma_start(tiles[b][:], src[b * P : (b + 1) * P, :])

        load_block(second_sb, second, 0)
        nc.sync.dma_start(slots[:], offs)
        for b in range(1, EB):
            load_block(second_sb, second, b)
        load_block(first_sb, first, 0)
        nc.sync.dma_start(places[:], offs2)
        for g in range(2):
            nc.sync.dma_start(ws_sb[g][:], ws_rows[:, :, g * HALF : (g + 1) * HALF])
        for b in range(1, EB):
            load_block(first_sb, first, b)
        nc.scalar.dma_start(bias_rows[0:JB, :], bias.rearrange("(b p) o -> b (p o)", p=P))

        width = {"vt": E, "ws0": HALF, "ws1": HALF}
        woven = {n: keep.tile([P, width[n] * PACK], BF16, name=f"{n}_woven", align_bytes=64) for n in width}
        codes = {n: keep.tile([P, width[n]], U32, name=f"{n}_codes", align_bytes=64) for n in width}
        scales = {n: keep.tile([P, width[n]], U8, name=f"{n}_scales", align_bytes=64) for n in width}
        gate = {(h, g): held.tile([P, BANK], F32, name=f"gate{h}{g}") for h in range(2) for g in range(2)}
        biased = {k: keep.tile([P, BANK], F32, name=f"biased{k[0]}{k[1]}") for k in gate}

        nc.tensor.transpose(gate[1, 1][:, 0:P], bias_rows[:], ident[:])
        bias_col = keep.tile([P, JB], F32, name="bias_col")
        nc.scalar.activation(bias_col[:], gate[1, 1][:, 0:JB], IDENTITY)
        out_v = out.rearrange("(b p) e -> p b e", p=P)

        def quantise(name):
            nc.vector.quantize_mx(codes[name][:].bitcast(FP8X4), scales[name][:], woven[name][:])

        def pick_second(b):
            picked = keep.tile([P, I], BF16, name=f"second_picked{b}")
            nc.vector.tensor_copy(picked[:], second_sb[b][:].indirect(slots[:]))
            words = picked[:].bitcast(F32)
            turned = rotating.tile([P, BANK], F32, name="bank")
            for u in range(2):
                nc.tensor.transpose(turned[:, u * P : (u + 1) * P], words[:, u : I // 2 : 2], ident[:])
            dst = woven["vt"][:].bitcast(F32)[:, b * 2 * P : (b + 1) * 2 * P]
            nc.scalar.copy(
                dst.rearrange("p (e u) -> p e u", u=2), turned[:, 0 : 2 * P].rearrange("p (u e) -> p e u", u=2)
            )

        def weave_ws(g):
            nc.scalar.copy(
                woven[f"ws{g}"][:].rearrange("p (c i t) -> p c t i", i=LINE, t=PACK),
                ws_sb[g][:].rearrange("p t (c i) -> p c t i", i=LINE),
            )

        def mix(h, g):
            sums = rotating.tile([P, BANK], F32, name="bank")
            features = slice(h * HALF, (h + 1) * HALF)
            for s in range(2):
                block = slice(s * P, (s + 1) * P)
                nc.tensor.matmul_mx(
                    sums[:, s * HALF : (s + 1) * HALF],
                    lhsT=codes[f"ws{g}"][:, block].bitcast(FP8X4),
                    lhsT_scale=scales[f"ws{g}"][:, block],
                    rhs=codes["vt"][:, features].bitcast(FP8X4),
                    rhs_scale=scales["vt"][:, features],
                    start=True,
                    stop=True,
                )
            for s in range(2):
                cols = slice(s * HALF, (s + 1) * HALF)
                jb = 2 * g + s
                nc.scalar.activation(biased[h, g][:, cols], sums[:, cols], IDENTITY, bias=bias_col[:, jb : jb + 1])

        def pick_first(b, jb0, jb1):
            picked = keep.tile([P, (jb1 - jb0) * P], F32, name=f"first_picked{b}_{jb0}")
            entries = places[:, jb0 * P // ENTRIES : jb1 * P // ENTRIES]
            nc.vector.tensor_copy(picked[:], first_sb[b][:].indirect(entries))
            for jb in range(jb0, jb1):
                c0 = (jb % 2) * HALF + (b % 2) * P
                src = picked[:, (jb - jb0) * P : (jb - jb0 + 1) * P]
                nc.tensor.transpose(gate[b // 2, jb // 2][:, c0 : c0 + P], src, ident[:])

        low_res = {g: keep.tile([P, 2, 2, P], F32, name=f"low_res{g}") for g in range(2)}

        def piece(tile, b):
            return tile[:].rearrange("p (s b e) -> p s b e", s=2, b=2)[:, :, b, :]

        def finish_low(engine, g, b, ut):
            engine.tensor_tensor(low_res[g][:, :, b, :], ut, piece(biased[0, g], b), MULT)

        def store_low(queue, g, b):
            queue.dma_start(out_v[:, 2 * g : 2 * g + 2, b * P : (b + 1) * P], low_res[g][:, :, b, :])

        def finish_high(jb):
            g, s = divmod(jb, 2)
            cols = slice(s * HALF, (s + 1) * HALF)
            res = keep.tile([P, HALF], F32, name=f"high_res{jb}")
            nc.vector.tensor_tensor(res[:], gate[1, g][:, cols], biased[1, g][:, cols], MULT)
            nc.sync.dma_start(out_v[:, jb : jb + 1, HALF:E], res[:].rearrange("p (s e) -> p s e", e=HALF))

        for b in range(EB):
            pick_second(b)
        pick_first(0, 0, JB)
        quantise("vt")
        weave_ws(0)
        weave_ws(1)

        ut_block0 = keep.tile([P, 2, 2, P], F32, name="ut_block0", tag="ws1")
        for g in range(2):
            nc.scalar.copy(ut_block0[:, g, :, :], piece(gate[0, g], 0))

        quantise("ws0")
        mix(0, 0)
        finish_low(nc.gpsimd, 0, 0, ut_block0[:, 0, :, :])
        store_low(nc.sync, 0, 0)
        mix(1, 0)

        pick_first(1, 0, JB)
        ut_block1 = keep.tile([P, 2, P], F32, name="ut_block1")
        nc.scalar.copy(ut_block1[:], piece(gate[0, 0], 1))
        finish_low(nc.gpsimd, 0, 1, ut_block1[:])
        store_low(nc.sync, 0, 1)

        quantise("ws1")
        mix(0, 1)
        finish_low(nc.gpsimd, 1, 0, ut_block0[:, 1, :, :])
        mix(1, 1)

        pick_first(2, 0, JB)
        pick_first(3, 0, JB // 2)
        pick_first(3, JB // 2, JB)
        finish_low(nc.vector, 1, 1, piece(gate[0, 1], 1))
        store_low(nc.sync, 1, 1)
        finish_high(0)
        store_low(nc.scalar, 1, 0)
        for jb in range(1, JB):
            finish_high(jb)
